import numpy as np
import ml_dtypes


def mxq(x, axis, fmt="e4m3"):
    dtype, down = {"e4m3": (ml_dtypes.float8_e4m3fn, 7), "e5m2": (ml_dtypes.float8_e5m2, 14)}[fmt]
    v = np.moveaxis(np.asarray(x, np.float32).astype(ml_dtypes.bfloat16).astype(np.float64), axis, -1)
    blocks = v.reshape(v.shape[:-1] + (-1, 32))
    amax = np.abs(blocks).max(-1, keepdims=True)
    byte = np.maximum(np.where(amax > 0, np.frexp(amax)[1] - 1 + 127, 0) - down, 1)
    scale = np.exp2(byte - 127.0)
    codes = (blocks / scale).astype(np.float32).astype(dtype).astype(np.float64)
    return np.moveaxis((codes * scale).reshape(v.shape), -1, axis)


WIDE = False


def mx_kscale(k):
    if not WIDE:
        return np.ones(k)
    levels = np.array([10, -10, 5, -5, 0])
    if k % 512:
        return np.exp2(np.random.permutation(np.resize(levels, k // 32))).repeat(32)
    a = np.empty((k // 512, 16))
    for p in range(k // 512):
        a[p, :8] = np.random.permutation(np.resize(levels, 8))
        for g in range(8):
            far = levels[np.abs(levels - a[p, g]) >= 10]
            a[p, g + 8] = far[np.random.randint(len(far))]
    return np.exp2(a.ravel()).repeat(32)


def f64(x):
    return np.asarray(x).astype(np.float64)


def striped(idx):
    return np.tile(idx.reshape(-1, 16).T, (8, 1)).astype(np.uint16)


def unstriped(offs):
    return offs[:16].T.reshape(-1).astype(np.int64)


E2M1 = np.array([0.0, 0.5, 1.0, 1.5, 2.0, 3.0, 4.0, 6.0, -0.0, -0.5, -1.0, -1.5, -2.0, -3.0, -4.0, -6.0])


def pack_weight(w, fmt):
    k, n = w.shape
    w = f64(np.asarray(w, np.float32).astype(ml_dtypes.bfloat16)).reshape(k // 32, 32, n)
    amax = np.abs(w).max(1)
    if fmt == "e4m3":
        byte = np.frexp(amax)[1] - 1 + 127 - 7
    else:
        mant, ex = np.frexp(amax / 6.0)
        byte = np.where(mant > 0.5, ex, ex - 1) + 127
    byte = np.clip(np.where(amax > 0, byte, 1), 1, 254)
    scaled = (w * np.exp2(127.0 - byte)[:, None, :]).reshape(k, n).astype(np.float32)
    by_word = np.ascontiguousarray(scaled.reshape(k // 512, 128, 4, n).transpose(0, 1, 3, 2))
    if fmt == "e4m3":
        words = by_word.astype(ml_dtypes.float8_e4m3fn).view(np.uint8)
    else:
        c = by_word.astype(ml_dtypes.float4_e2m1fn).view(np.uint8) & 0xF
        words = (c[..., 0::2] | (c[..., 1::2] << 4)).reshape(k // 512, 128, 2 * n)
    return np.ascontiguousarray(words), np.ascontiguousarray(byte.astype(np.uint8).reshape(k // 512, 16, n))


def unpack_weight(words, scales, fmt):
    g, _, n = scales.shape
    words = np.ascontiguousarray(words).reshape(g, 128, n, -1)
    if fmt == "e4m3":
        vals = words.view(ml_dtypes.float8_e4m3fn).astype(np.float64)
    else:
        nib = np.empty((g, 128, n, 4), np.uint8)
        nib[..., 0::2] = words & 0xF
        nib[..., 1::2] = words >> 4
        vals = E2M1[nib]
    vals = vals * np.repeat(np.exp2(scales.astype(np.float64) - 127.0), 8, axis=1)[..., None]
    return vals.transpose(0, 1, 3, 2).reshape(g * 512, n)


def gelu(v):
    return 0.5 * v * (1.0 + np.tanh(np.sqrt(2.0 / np.pi) * (v + 0.044715 * v**3)))


K, K2, H, N, T, T2, S, P = 512, 1024, 1024, 768, 4096, 2048, 1024, 512


def setup_inputs():
    n = np.random.standard_normal
    s = mx_kscale(K)[:, None]
    s2 = mx_kscale(K2)[:, None]
    u = mx_kscale(H)[:, None]
    tab_words, tab_scales = pack_weight(n((K, T)) * s, "e4m3")
    tab2_words, tab2_scales = pack_weight(n((K2, T2)) * s2, "e4m3")
    w2_words, w2_scales = pack_weight(n((K, H)) / np.sqrt(K) / s * u.T, "e2m1")
    w4_words, w4_scales = pack_weight(0.55 * n((K2, N)) / np.sqrt(K2) / s2, "e4m3")
    return {
        "tab_words": tab_words, "tab_scales": tab_scales,
        "tab2_words": tab2_words, "tab2_scales": tab2_scales,
        "offs": striped(np.random.permutation(T)[:S]),
        "offs2": striped(np.random.permutation(T2)[:P]),
        "pos1": striped(np.random.permutation(S)[:P]),
        "w1": (n((K, H)) / np.sqrt(K) / s * u.T).astype(np.float32),
        "w2_words": w2_words, "w2_scales": w2_scales,
        "store": (0.7 * n((H, S)) * u).astype(np.float32),
        "w3": (0.35 * n((H, N)) / np.sqrt(H) / u).astype(np.float32),
        "w4_words": w4_words, "w4_scales": w4_scales,
    }


def reference(tab_words, tab_scales, tab2_words, tab2_scales, offs, offs2, pos1,
              w1, w2_words, w2_scales, store, w3, w4_words, w4_scales):
    v = unpack_weight(tab_words, tab_scales, "e4m3")[:, unstriped(offs)]
    v2 = unpack_weight(tab2_words, tab2_scales, "e4m3")[:, unstriped(offs2)]
    w2 = unpack_weight(w2_words, w2_scales, "e2m1")
    w4 = unpack_weight(w4_words, w4_scales, "e4m3")
    d1 = mxq(f64(w1), 0, "e4m3").T @ v
    d2 = w2.T @ v
    h = np.minimum(d1, d2) + f64(store)
    y = mxq(f64(w3), 0, "e4m3").T @ mxq(h, 0, "e4m3")
    b = w4.T @ v2
    return y[:, unstriped(pos1)] - np.sin(b)

@@ -1,0 +1,308 @@
+import math
+from contextlib import ExitStack
+
+import concourse.mybir as mybir
+
+K, K2, H, N, T, T2, S, B = 512, 1024, 1024, 768, 4096, 2048, 1024, 512
+FLOPS = 2 * (2 * K * H * S + H * N * S + K2 * N * B)
+
+F32 = mybir.dt.float32
+BF16 = mybir.dt.bfloat16
+I32 = mybir.dt.int32
+U32 = mybir.dt.uint32
+U16 = mybir.dt.uint16
+U8 = mybir.dt.uint8
+FP8X4 = mybir.dt.float8_e4m3fn_x4
+FP4X4 = mybir.dt.float4_e2m1fn_x4
+ALU = mybir.AluOpType
+ACT = mybir.ActivationFunctionType
+
+P = 128
+PACK = 4
+PASS = P * PACK
+BANK = 512
+QUADS = 4
+LIST_COLS = BANK // 16
+N_TILES = N // P
+W3_PIECE = 384
+W1_PIECE = 256
+QUARTER = 0.75
+PLANE2 = 8
+
+
+def tile_list_bag_stability_features_kernel(
+    tc, tab_words, tab_scales, tab2_words, tab2_scales, offs, offs2, pos1,
+    w1, w2_words, w2_scales, store, w3, w4_words, w4_scales, out,
+):
+    nc = tc.nc
+    with ExitStack() as ctx:
+        keep = ctx.enter_context(tc.tile_pool(name="keep", bufs=1))
+        two = ctx.enter_context(tc.tile_pool(name="two", bufs=2))
+        three = ctx.enter_context(tc.tile_pool(name="three", bufs=3))
+        psum_d = ctx.enter_context(tc.psum_pool(name="psum_d", bufs=3))
+        psum_acc = ctx.enter_context(tc.psum_pool(name="psum_acc", bufs=2))
+
+        def kept(shape, dtype, name):
+            return keep.tile(shape, dtype, name=name, align_bytes=64)
+
+        def load_scales(clear, queue, plane, scales, first):
+            rows = PACK * scales.shape[0]
+            clear.memset(plane[:].bitcast(I32), 0)
+            for q in range(QUADS):
+                queue.dma_start(
+                    out=plane[32 * q + first : 32 * q + first + rows, :].bitcast(I32),
+                    in_=scales[:, 4 * q : 4 * q + 4, :].bitcast(I32),
+                )
+
+        def load_words(tile, words):
+            nc.sync.dma_start(out=tile.bitcast(I32), in_=words.rearrange("p t i -> p (t i)").bitcast(I32))
+
+        def load_rows(pool, rows, name, tag):
+            raw = pool.tile([P, PACK, rows.shape[1]], F32, name=name, tag=tag)
+            nc.sync.dma_start(out=raw[:], in_=rows.rearrange("(p j) c -> p j c", j=PACK))
+            return raw
+
+        def load_w1(g):
+            return [
+                load_rows(keep, w1[:, g * PASS + e * W1_PIECE : g * PASS + (e + 1) * W1_PIECE], "w1_raw", "w1_raw%d%d" % (g, e))
+                for e in range(PASS // W1_PIECE)
+            ]
+
+        def load_store(half, g):
+            rows = store[g * PASS : (g + 1) * PASS, half * BANK : (half + 1) * BANK]
+            return load_rows(three, rows, "store_sb", "store_sb")
+
+        def load_w3(g):
+            return [
+                load_rows(three, w3[g * PASS : (g + 1) * PASS, e * W3_PIECE : (e + 1) * W3_PIECE], "w3_raw", "w3_raw")
+                for e in range(N // W3_PIECE)
+            ]
+
+        idx = kept([P, S // 16], U16, "idx")
+        idx2 = kept([P, B // 16], U16, "idx2")
+        picks = kept([P, B // 16], U16, "picks")
+        nc.sync.dma_start(idx[:], offs)
+        nc.sync.dma_start(idx2[:], offs2)
+        nc.sync.dma_start(picks[:], pos1)
+        w2_raw = kept([P, 2 * H], U8, "w2_raw")
+        nc.sync.dma_start(out=w2_raw[:].bitcast(I32), in_=w2_words[0].bitcast(I32))
+        tab_w = kept([P, T], U32, "tab_w")
+        for e in range(2):
+            cols = slice(e * T // 2, (e + 1) * T // 2)
+            load_words(tab_w[:, cols], tab_words[0, :, cols, :])
+        w1_raw = [load_w1(0)]
+
+        tab_s = kept([P, T], U8, "tab_s")
+        w2_s_raw = kept([P, H], U8, "w2_s_raw")
+        tab2_s = kept([P, T2], U8, "tab2_s")
+        w4_s = kept([P, N], U8, "w4_s")
+        load_scales(nc.vector, nc.scalar, tab_s, tab_scales, 0)
+        load_scales(nc.gpsimd, nc.gpsimd, w2_s_raw, w2_scales, 0)
+        load_scales(nc.vector, nc.gpsimd, tab2_s, tab2_scales, PLANE2)
+        load_scales(nc.vector, nc.gpsimd, w4_s, w4_scales, PLANE2)
+
+        store_sb = {}
+        store_sb[0, 0] = load_store(0, 0)
+        store_sb[1, 0] = load_store(1, 0)
+        w1_raw.append(load_w1(1))
+        w3_raw = [load_w3(0)]
+        tab2_w = [kept([P, T2], U32, "tab2_w%d" % a) for a in range(2)]
+        w4_w = [kept([P, N], U32, "w4_w%d" % a) for a in range(2)]
+        for a in range(2):
+            load_words(tab2_w[a][:], tab2_words[a])
+        for a in range(2):
+            load_words(w4_w[a][:], w4_words[a])
+        store_sb[0, 1] = load_store(0, 1)
+
+        w2_w = kept([P, 2 * H], U8, "w2_w")
+        w2_s = kept([P, H], U8, "w2_s")
+        nc.vector.tensor_copy(
+            out=w2_w[:].rearrange("p (g t m b) -> p g t m b", g=2, t=PACK, b=2),
+            in_=w2_raw[:].rearrange("p (g m t b) -> p g t m b", g=2, t=PACK, b=2),
+        )
+        nc.vector.tensor_copy(
+            out=w2_s[:].rearrange("p (g t m) -> p g t m", g=2, t=PACK),
+            in_=w2_s_raw[:].rearrange("p (g m t) -> p g t m", g=2, t=PACK),
+        )
+
+        v_w = [kept([P, BANK], U32, "v_w%d" % i) for i in range(2)]
+        v_s = [kept([P, BANK], U8, "v_s%d" % i) for i in range(2)]
+
+        def gather_v(out_tile, window, half):
+            nc.vector.tensor_copy(out_tile[:], window[:].indirect(idx[:, half * LIST_COLS : (half + 1) * LIST_COLS]))
+
+        w1_w = [kept([P, PASS], U32, "w1_w%d" % g) for g in range(2)]
+        w1_s = [kept([P, PASS], U8, "w1_s%d" % g) for g in range(2)]
+
+        w1_bf = {}
+
+        def round_w1(g, e):
+            if e == 0:
+                w1_bf[g] = three.tile([P, PACK * PASS], BF16, name="grouped", tag="grouped", align_bytes=64)
+            m = slice(e * W1_PIECE // PACK, (e + 1) * W1_PIECE // PACK)
+            nc.scalar.copy(
+                out=w1_bf[g][:].rearrange("p (t m j) -> p m j t", t=PACK, j=PACK)[:, m, :, :],
+                in_=w1_raw[g][e][:].rearrange("p j (m t) -> p m j t", t=PACK),
+            )
+
+        def quantize_w1(g):
+            nc.vector.quantize_mx(out=w1_w[g][:].bitcast(FP8X4), scales=w1_s[g][:], in_=w1_bf[g][:])
+
+        w3_w = [kept([P, N], U32, "w3_w%d" % g) for g in range(2)]
+        w3_s = [kept([P, N], U8, "w3_s%d" % g) for g in range(2)]
+
+        w3_bf = {}
+
+        def round_w3(g, e):
+            w3_bf[g, e] = three.tile([P, PACK * W3_PIECE], BF16, name="grouped3", tag="grouped", align_bytes=64)
+            nc.scalar.copy(
+                out=w3_bf[g, e][:].rearrange("p (c i j) -> p c j i", i=4, j=PACK),
+                in_=w3_raw[g][e][:].rearrange("p j (c i) -> p c j i", i=4),
+            )
+
+        def quantize_w3(g, e):
+            cols = slice(e * W3_PIECE, (e + 1) * W3_PIECE)
+            nc.vector.quantize_mx(out=w3_w[g][:, cols].bitcast(FP8X4), scales=w3_s[g][:, cols], in_=w3_bf[g, e][:])
+
+        lesser = {}
+        h_bf = {}
+        h_w = {}
+        h_s = {}
+
+        def lesser_slice(half, g, t):
+            if t == 0:
+                lesser[half, g] = two.tile([P, PACK, BANK], F32, name="lesser", tag="lesser")
+            cols = slice(t * P, (t + 1) * P)
+            c = PACK * g + t
+            d1 = psum_d.tile([P, BANK], F32, name="d1", tag="d1")
+            nc.tensor.matmul_mx(
+                out=d1[:], lhsT=w1_w[g][:, cols].bitcast(FP8X4), lhsT_scale=w1_s[g][:, cols],
+                rhs=v_w[half][:].bitcast(FP8X4), rhs_scale=v_s[half][:], start=True, stop=True,
+            )
+            d2 = psum_d.tile([P, BANK], F32, name="d2", tag="d2")
+            nc.tensor.matmul_mx(
+                out=d2[:], lhsT=w2_w[:, 2 * P * c : 2 * P * (c + 1)].bitcast(FP4X4),
+                lhsT_scale=w2_s[:, P * c : P * (c + 1)],
+                rhs=v_w[half][:].bitcast(FP8X4), rhs_scale=v_s[half][:], start=True, stop=True,
+            )
+            row = lesser[half, g][:, t, :]
+            nc.scalar.copy(out=row, in_=d1[:])
+            nc.vector.tensor_tensor(out=row, in0=d2[:], in1=row, op=ALU.min)
+
+        def add_store(half, g):
+            h_bf[half, g] = two.tile([P, PACK * BANK], BF16, name="h_bf", tag="h_bf", align_bytes=64)
+            nc.vector.tensor_tensor(
+                out=h_bf[half, g][:].rearrange("p (c i t) -> p c t i", i=2, t=PACK),
+                in0=lesser[half, g][:].rearrange("p t (c i) -> p c t i", i=2),
+                in1=store_sb[half, g][:].rearrange("p t (c i) -> p c t i", i=2),
+                op=ALU.add,
+            )
+
+        def quantize_h(half, g):
+            h_w[half, g] = kept([P, BANK], U32, "h_w%d%d" % (half, g))
+            h_s[half, g] = kept([P, BANK], U8, "h_s%d%d" % (half, g))
+            nc.vector.quantize_mx(out=h_w[half, g][:].bitcast(FP8X4), scales=h_s[half, g][:], in_=h_bf[half, g][:])
+
+        y_sb = [kept([P, S], F32, "y%d" % i) for i in range(N_TILES)]
+
+        def y_tile(i, half):
+            cols = slice(i * P, (i + 1) * P)
+            acc = psum_acc.tile([P, BANK], F32, name="acc", tag="acc")
+            for g in range(2):
+                nc.tensor.matmul_mx(
+                    out=acc[:], lhsT=w3_w[g][:, cols].bitcast(FP8X4), lhsT_scale=w3_s[g][:, cols],
+                    rhs=h_w[half, g][:].bitcast(FP8X4), rhs_scale=h_s[half, g][:],
+                    start=(g == 0), stop=(g == 1),
+                )
+            nc.scalar.copy(out=y_sb[i][:, half * BANK : (half + 1) * BANK], in_=acc[:])
+
+        v2_w = [kept([P, B], U32, "v2_w%d" % a) for a in range(2)]
+        v2_s = kept([P, B], U8, "v2_s")
+
+        def gather_v2():
+            nc.vector.tensor_copy(v2_s[:], tab2_s[:].indirect(idx2[:]))
+            for a in range(2):
+                nc.vector.tensor_copy(v2_w[a][:], tab2_w[a][:].indirect(idx2[:]))
+
+        sine = [kept([P, B], F32, "sine%d" % i) for i in range(N_TILES)]
+        turns = {}
+        whole = {}
+
+        def b_tile(i):
+            cols = slice(i * P, (i + 1) * P)
+            acc = psum_acc.tile([P, BANK], F32, name="acc", tag="acc")
+            for a in range(2):
+                nc.tensor.matmul_mx(
+                    out=acc[:], lhsT=w4_w[a][:, cols].bitcast(FP8X4), lhsT_scale=w4_s[PLANE2 + PACK * a : P, cols],
+                    rhs=v2_w[a][:].bitcast(FP8X4), rhs_scale=v2_s[PLANE2 + PACK * a : P, :],
+                    start=(a == 0), stop=(a == 1),
+                )
+            turns[i] = three.tile([P, B], F32, name="turns", tag="turns")
+            nc.scalar.activation(out=turns[i][:], in_=acc[:], func=ACT.Abs, scale=1.0 / (2.0 * math.pi), bias=QUARTER)
+            whole[i] = three.tile([P, B], U32, name="whole", tag="whole")
+            nc.scalar.activation(out=whole[i][:], in_=turns[i][:], func=ACT.Copy, bias=-0.25)
+
+        def sine_tile(i):
+            nc.vector.tensor_tensor(out=turns[i][:], in0=turns[i][:], in1=whole[i][:].bitcast(I32), op=ALU.subtract)
+            nc.scalar.activation(out=sine[i][:], in_=turns[i][:], func=ACT.Sin, scale=-2.0 * math.pi, bias=math.pi / 2.0)
+
+        def out_tile(i):
+            result = three.tile([P, B], F32, name="result", tag="result")
+            nc.vector.tensor_tensor(out=result[:], in0=y_sb[i][:].indirect(picks[:]), in1=sine[i][:], op=ALU.subtract)
+            nc.sync.dma_start(out=out[i * P : (i + 1) * P, :], in_=result[:])
+
+        gather_v(v_w[0], tab_w, 0)
+        gather_v(v_s[0], tab_s, 0)
+        round_w1(0, 0)
+        round_w1(0, 1)
+        gather_v(v_w[1], tab_w, 1)
+        quantize_w1(0)
+        gather_v(v_s[1], tab_s, 1)
+        for t in range(PACK):
+            lesser_slice(0, 0, t)
+        lesser_slice(1, 0, 0)
+        add_store(0, 0)
+        store_sb[1, 1] = load_store(1, 1)
+        lesser_slice(1, 0, 1)
+        round_w1(1, 0)
+        quantize_h(0, 0)
+        lesser_slice(1, 0, 2)
+        round_w1(1, 1)
+        lesser_slice(1, 0, 3)
+        quantize_w1(1)
+        round_w3(0, 0)
+        add_store(1, 0)
+        lesser_slice(0, 1, 0)
+        round_w3(0, 1)
+        w3_raw.append(load_w3(1))
+        quantize_h(1, 0)
+        gather_v2()
+        for t in range(1, PACK):
+            lesser_slice(0, 1, t)
+        quantize_w3(0, 0)
+        quantize_w3(0, 1)
+        lesser_slice(1, 1, 0)
+        b_tile(0)
+        add_store(0, 1)
+        lesser_slice(1, 1, 1)
+        b_tile(1)
+        quantize_h(0, 1)
+        lesser_slice(1, 1, 2)
+        b_tile(2)
+        lesser_slice(1, 1, 3)
+        round_w3(1, 0)
+        round_w3(1, 1)
+        sine_tile(0)
+        sine_tile(1)
+        sine_tile(2)
+        add_store(1, 1)
+        quantize_w3(1, 0)
+        quantize_h(1, 1)
+        quantize_w3(1, 1)
+        for i in range(N_TILES):
+            y_tile(i, 0)
+            y_tile(i, 1)
+            if i + 3 < N_TILES:
+                b_tile(i + 3)
+                sine_tile(i + 3)
+            out_tile(i)

@@ -24,9 +24,11 @@ BANK = 512
 QUADS = 4
 LIST_COLS = BANK // 16
 N_TILES = N // P
-W3_PIECE = 384
+W3_CUTS = (0, 512, 768)
 W1_PIECE = 256
-QUARTER = 0.75
+CAST = 256
+TAB_CUTS = tuple(range(0, T + 1, 512))
+QUARTER = -0.25
 PLANE2 = 8
 
 
@@ -39,6 +41,7 @@ def tile_list_bag_stability_features_kernel(
         keep = ctx.enter_context(tc.tile_pool(name="keep", bufs=1))
         two = ctx.enter_context(tc.tile_pool(name="two", bufs=2))
         three = ctx.enter_context(tc.tile_pool(name="three", bufs=3))
+        four = ctx.enter_context(tc.tile_pool(name="four", bufs=4))
         psum_d = ctx.enter_context(tc.psum_pool(name="psum_d", bufs=3))
         psum_acc = ctx.enter_context(tc.psum_pool(name="psum_acc", bufs=2))
 
@@ -54,6 +57,11 @@ def tile_list_bag_stability_features_kernel(
                     in_=scales[:, 4 * q : 4 * q + 4, :].bitcast(I32),
                 )
 
+        def load_scale_rows(clear, plane, scales):
+            clear.memset(plane[:].bitcast(I32), 0)
+            for r in range(PACK):
+                nc.sync.dma_start(out=plane[r:P:32, :].bitcast(I32), in_=scales[0, r:16:PACK, :].bitcast(I32))
+
         def load_words(tile, words):
             nc.sync.dma_start(out=tile.bitcast(I32), in_=words.rearrange("p t i -> p (t i)").bitcast(I32))
 
@@ -64,7 +72,7 @@ def tile_list_bag_stability_features_kernel(
 
         def load_w1(g):
             return [
-                load_rows(keep, w1[:, g * PASS + e * W1_PIECE : g * PASS + (e + 1) * W1_PIECE], "w1_raw", "w1_raw%d%d" % (g, e))
+                load_rows(four, w1[:, g * PASS + e * W1_PIECE : g * PASS + (e + 1) * W1_PIECE], "w1_raw", "w1_raw")
                 for e in range(PASS // W1_PIECE)
             ]
 
@@ -72,11 +80,9 @@ def tile_list_bag_stability_features_kernel(
             rows = store[g * PASS : (g + 1) * PASS, half * BANK : (half + 1) * BANK]
             return load_rows(three, rows, "store_sb", "store_sb")
 
-        def load_w3(g):
-            return [
-                load_rows(three, w3[g * PASS : (g + 1) * PASS, e * W3_PIECE : (e + 1) * W3_PIECE], "w3_raw", "w3_raw")
-                for e in range(N // W3_PIECE)
-            ]
+        def load_w3(g, e):
+            rows = w3[g * PASS : (g + 1) * PASS, W3_CUTS[e] : W3_CUTS[e + 1]]
+            return load_rows(two, rows, "w3_raw", "w3_raw") if e == 0 else load_rows(four, rows, "w3_raw", "w1_raw")
 
         idx = kept([P, S // 16], U16, "idx")
         idx2 = kept([P, B // 16], U16, "idx2")
@@ -86,50 +92,55 @@ def tile_list_bag_stability_features_kernel(
         nc.sync.dma_start(picks[:], pos1)
         w2_raw = kept([P, 2 * H], U8, "w2_raw")
         nc.sync.dma_start(out=w2_raw[:].bitcast(I32), in_=w2_words[0].bitcast(I32))
+        w2_s_raw = kept([P, H], U8, "w2_s_raw")
+        load_scale_rows(nc.vector, w2_s_raw, w2_scales)
+        warm = kept([P, 1], F32, "warm")
+        nc.gpsimd.memset(warm[:], 0.0)
+        warm_out = kept([P, 1], F32, "warm_out")
+        nc.scalar.activation(out=warm_out[:], in_=warm[:], func=ACT.Sin)
+
         tab_w = kept([P, T], U32, "tab_w")
-        for e in range(2):
-            cols = slice(e * T // 2, (e + 1) * T // 2)
+        for e in range(len(TAB_CUTS) - 1):
+            cols = slice(TAB_CUTS[e], TAB_CUTS[e + 1])
             load_words(tab_w[:, cols], tab_words[0, :, cols, :])
-        w1_raw = [load_w1(0)]
 
         tab_s = kept([P, T], U8, "tab_s")
-        w2_s_raw = kept([P, H], U8, "w2_s_raw")
         tab2_s = kept([P, T2], U8, "tab2_s")
         w4_s = kept([P, N], U8, "w4_s")
-        load_scales(nc.vector, nc.scalar, tab_s, tab_scales, 0)
-        load_scales(nc.gpsimd, nc.gpsimd, w2_s_raw, w2_scales, 0)
-        load_scales(nc.vector, nc.gpsimd, tab2_s, tab2_scales, PLANE2)
-        load_scales(nc.vector, nc.gpsimd, w4_s, w4_scales, PLANE2)
+        load_scale_rows(nc.vector, tab_s, tab_scales)
+        w1_raw = [load_w1(0)]
 
         store_sb = {}
-        store_sb[0, 0] = load_store(0, 0)
-        store_sb[1, 0] = load_store(1, 0)
-        w1_raw.append(load_w1(1))
-        w3_raw = [load_w3(0)]
+        w3_raw = {}
         tab2_w = [kept([P, T2], U32, "tab2_w%d" % a) for a in range(2)]
         w4_w = [kept([P, N], U32, "w4_w%d" % a) for a in range(2)]
-        for a in range(2):
-            load_words(tab2_w[a][:], tab2_words[a])
+
+        load_scales(nc.vector, nc.sync, tab2_s, tab2_scales, PLANE2)
+        store_sb[0, 0] = load_store(0, 0)
+        load_words(tab2_w[0][:], tab2_words[0])
+        w1_raw.append(load_w1(1))
+        load_words(tab2_w[1][:], tab2_words[1])
+        load_scales(nc.vector, nc.sync, w4_s, w4_scales, PLANE2)
         for a in range(2):
             load_words(w4_w[a][:], w4_words[a])
+        store_sb[1, 0] = load_store(1, 0)
+        w3_raw[0, 0] = load_w3(0, 0)
         store_sb[0, 1] = load_store(0, 1)
-
+        w3_raw[1, 0] = load_w3(1, 0)
         w2_w = kept([P, 2 * H], U8, "w2_w")
         w2_s = kept([P, H], U8, "w2_s")
         nc.vector.tensor_copy(
             out=w2_w[:].rearrange("p (g t m b) -> p g t m b", g=2, t=PACK, b=2),
             in_=w2_raw[:].rearrange("p (g m t b) -> p g t m b", g=2, t=PACK, b=2),
         )
-        nc.vector.tensor_copy(
-            out=w2_s[:].rearrange("p (g t m) -> p g t m", g=2, t=PACK),
-            in_=w2_s_raw[:].rearrange("p (g m t) -> p g t m", g=2, t=PACK),
-        )
 
-        v_w = [kept([P, BANK], U32, "v_w%d" % i) for i in range(2)]
-        v_s = [kept([P, BANK], U8, "v_s%d" % i) for i in range(2)]
+        v_w = {}
+        v_s = {}
 
-        def gather_v(out_tile, window, half):
-            nc.vector.tensor_copy(out_tile[:], window[:].indirect(idx[:, half * LIST_COLS : (half + 1) * LIST_COLS]))
+        def gather_v(window, half, dtype, tag):
+            picked = keep.tile([P, BANK], dtype, name="picked", tag=tag, align_bytes=64)
+            nc.vector.tensor_copy(picked[:], window[:].indirect(idx[:, half * LIST_COLS : (half + 1) * LIST_COLS]))
+            return picked
 
         w1_w = [kept([P, PASS], U32, "w1_w%d" % g) for g in range(2)]
         w1_s = [kept([P, PASS], U8, "w1_s%d" % g) for g in range(2)]
@@ -138,7 +149,7 @@ def tile_list_bag_stability_features_kernel(
 
         def round_w1(g, e):
             if e == 0:
-                w1_bf[g] = three.tile([P, PACK * PASS], BF16, name="grouped", tag="grouped", align_bytes=64)
+                w1_bf[g] = keep.tile([P, PACK * PASS], BF16, name="w1_bf", tag="w1_bf%d" % g, align_bytes=64)
             m = slice(e * W1_PIECE // PACK, (e + 1) * W1_PIECE // PACK)
             nc.scalar.copy(
                 out=w1_bf[g][:].rearrange("p (t m j) -> p m j t", t=PACK, j=PACK)[:, m, :, :],
@@ -153,15 +164,17 @@ def tile_list_bag_stability_features_kernel(
 
         w3_bf = {}
 
-        def round_w3(g, e):
-            w3_bf[g, e] = three.tile([P, PACK * W3_PIECE], BF16, name="grouped3", tag="grouped", align_bytes=64)
-            nc.scalar.copy(
-                out=w3_bf[g, e][:].rearrange("p (c i j) -> p c j i", i=4, j=PACK),
-                in_=w3_raw[g][e][:].rearrange("p j (c i) -> p c j i", i=4),
-            )
+        def round_w3(g, e, copy):
+            width = W3_CUTS[e + 1] - W3_CUTS[e]
+            w3_bf[g, e] = two.tile([P, PACK * width], BF16, name="grouped3", tag="grouped", align_bytes=64)
+            for c0 in range(0, width, CAST):
+                copy(
+                    out=w3_bf[g, e][:, PACK * c0 : PACK * (c0 + CAST)].rearrange("p (c i j) -> p c j i", i=4, j=PACK),
+                    in_=w3_raw[g, e][:, :, c0 : c0 + CAST].rearrange("p j (c i) -> p c j i", i=4),
+                )
 
         def quantize_w3(g, e):
-            cols = slice(e * W3_PIECE, (e + 1) * W3_PIECE)
+            cols = slice(W3_CUTS[e], W3_CUTS[e + 1])
             nc.vector.quantize_mx(out=w3_w[g][:, cols].bitcast(FP8X4), scales=w3_s[g][:, cols], in_=w3_bf[g, e][:])
 
         lesser = {}
@@ -171,7 +184,7 @@ def tile_list_bag_stability_features_kernel(
 
         def lesser_slice(half, g, t):
             if t == 0:
-                lesser[half, g] = two.tile([P, PACK, BANK], F32, name="lesser", tag="lesser")
+                lesser[half, g] = three.tile([P, PACK, BANK], F32, name="lesser", tag="lesser")
             cols = slice(t * P, (t + 1) * P)
             c = PACK * g + t
             d1 = psum_d.tile([P, BANK], F32, name="d1", tag="d1")
@@ -205,9 +218,9 @@ def tile_list_bag_stability_features_kernel(
 
         y_sb = [kept([P, S], F32, "y%d" % i) for i in range(N_TILES)]
 
-        def y_tile(i, half):
+        def y_tile(i, half, pool, tag):
             cols = slice(i * P, (i + 1) * P)
-            acc = psum_acc.tile([P, BANK], F32, name="acc", tag="acc")
+            acc = pool.tile([P, BANK], F32, name="y_acc", tag=tag)
             for g in range(2):
                 nc.tensor.matmul_mx(
                     out=acc[:], lhsT=w3_w[g][:, cols].bitcast(FP8X4), lhsT_scale=w3_s[g][:, cols],
@@ -217,14 +230,12 @@ def tile_list_bag_stability_features_kernel(
             nc.scalar.copy(out=y_sb[i][:, half * BANK : (half + 1) * BANK], in_=acc[:])
 
         v2_w = [kept([P, B], U32, "v2_w%d" % a) for a in range(2)]
-        v2_s = kept([P, B], U8, "v2_s")
+        v2_s = {}
 
         def gather_v2():
-            nc.vector.tensor_copy(v2_s[:], tab2_s[:].indirect(idx2[:]))
             for a in range(2):
                 nc.vector.tensor_copy(v2_w[a][:], tab2_w[a][:].indirect(idx2[:]))
 
-        sine = [kept([P, B], F32, "sine%d" % i) for i in range(N_TILES)]
         turns = {}
         whole = {}
 
@@ -234,75 +245,110 @@ def tile_list_bag_stability_features_kernel(
             for a in range(2):
                 nc.tensor.matmul_mx(
                     out=acc[:], lhsT=w4_w[a][:, cols].bitcast(FP8X4), lhsT_scale=w4_s[PLANE2 + PACK * a : P, cols],
-                    rhs=v2_w[a][:].bitcast(FP8X4), rhs_scale=v2_s[PLANE2 + PACK * a : P, :],
+                    rhs=v2_w[a][:].bitcast(FP8X4), rhs_scale=v2_s[0][PLANE2 + PACK * a : P, :],
                     start=(a == 0), stop=(a == 1),
                 )
-            turns[i] = three.tile([P, B], F32, name="turns", tag="turns")
+            turns[i] = kept([P, B], F32, "turns%d" % i)
             nc.scalar.activation(out=turns[i][:], in_=acc[:], func=ACT.Abs, scale=1.0 / (2.0 * math.pi), bias=QUARTER)
             whole[i] = three.tile([P, B], U32, name="whole", tag="whole")
             nc.scalar.activation(out=whole[i][:], in_=turns[i][:], func=ACT.Copy, bias=-0.25)
 
         def sine_tile(i):
             nc.vector.tensor_tensor(out=turns[i][:], in0=turns[i][:], in1=whole[i][:].bitcast(I32), op=ALU.subtract)
-            nc.scalar.activation(out=sine[i][:], in_=turns[i][:], func=ACT.Sin, scale=-2.0 * math.pi, bias=math.pi / 2.0)
+
+        def sine_of(i):
+            nc.scalar.activation(out=turns[i][:], in_=turns[i][:], func=ACT.Sin, scale=-2.0 * math.pi, bias=math.pi / 2.0)
 
         def out_tile(i):
-            result = three.tile([P, B], F32, name="result", tag="result")
-            nc.vector.tensor_tensor(out=result[:], in0=y_sb[i][:].indirect(picks[:]), in1=sine[i][:], op=ALU.subtract)
+            result = three.tile([P, B], F32, name="result", tag="result" if i < 3 else "whole")
+            nc.vector.tensor_tensor(out=result[:], in0=y_sb[i][:].indirect(picks[:]), in1=turns[i][:], op=ALU.subtract)
             nc.sync.dma_start(out=out[i * P : (i + 1) * P, :], in_=result[:])
 
-        gather_v(v_w[0], tab_w, 0)
-        gather_v(v_s[0], tab_s, 0)
+        v_w[0] = gather_v(tab_w, 0, U32, "v_w0")
+        v_s[0] = gather_v(tab_s, 0, U8, "v_s0")
         round_w1(0, 0)
         round_w1(0, 1)
-        gather_v(v_w[1], tab_w, 1)
         quantize_w1(0)
-        gather_v(v_s[1], tab_s, 1)
-        for t in range(PACK):
-            lesser_slice(0, 0, t)
+        nc.vector.tensor_copy(
+            out=w2_s[:].rearrange("p (g t m) -> p g t m", g=2, t=PACK),
+            in_=w2_s_raw[:].rearrange("p (g m t) -> p g t m", g=2, t=PACK),
+        )
+        v_w[1] = gather_v(tab_w, 1, U32, "v_w1")
+        v_s[1] = gather_v(tab_s, 1, U8, "v_s1")
+        v2_s[0] = keep.tile([P, B], U8, name="v2_s", tag="w1_bf0", align_bytes=64)
+        nc.vector.tensor_copy(v2_s[0][:], tab2_s[:].indirect(idx2[:]))
+        lesser_slice(0, 0, 0)
+        lesser_slice(0, 0, 1)
+        lesser_slice(0, 0, 2)
+        lesser_slice(0, 0, 3)
         lesser_slice(1, 0, 0)
+        lesser_slice(1, 0, 1)
+        lesser_slice(1, 0, 2)
+        lesser_slice(1, 0, 3)
+        round_w1(1, 0)
+        round_w1(1, 1)
         add_store(0, 0)
         store_sb[1, 1] = load_store(1, 1)
-        lesser_slice(1, 0, 1)
-        round_w1(1, 0)
-        quantize_h(0, 0)
-        lesser_slice(1, 0, 2)
-        round_w1(1, 1)
-        lesser_slice(1, 0, 3)
+        w3_raw[0, 1] = load_w3(0, 1)
+        w3_raw[1, 1] = load_w3(1, 1)
         quantize_w1(1)
-        round_w3(0, 0)
-        add_store(1, 0)
-        lesser_slice(0, 1, 0)
-        round_w3(0, 1)
-        w3_raw.append(load_w3(1))
-        quantize_h(1, 0)
+        quantize_h(0, 0)
         gather_v2()
-        for t in range(1, PACK):
-            lesser_slice(0, 1, t)
-        quantize_w3(0, 0)
-        quantize_w3(0, 1)
+        lesser_slice(0, 1, 0)
+        lesser_slice(0, 1, 1)
+        lesser_slice(0, 1, 2)
+        lesser_slice(0, 1, 3)
+        add_store(1, 0)
+        quantize_h(1, 0)
         lesser_slice(1, 1, 0)
-        b_tile(0)
-        add_store(0, 1)
         lesser_slice(1, 1, 1)
-        b_tile(1)
-        quantize_h(0, 1)
         lesser_slice(1, 1, 2)
-        b_tile(2)
         lesser_slice(1, 1, 3)
-        round_w3(1, 0)
-        round_w3(1, 1)
+        b_tile(0)
+        b_tile(1)
+        b_tile(2)
+        round_w3(0, 0, nc.scalar.copy)
+        round_w3(1, 0, nc.scalar.copy)
         sine_tile(0)
         sine_tile(1)
         sine_tile(2)
-        add_store(1, 1)
+        quantize_w3(0, 0)
+        add_store(0, 1)
         quantize_w3(1, 0)
+        quantize_h(0, 1)
+        b_tile(3)
+        b_tile(4)
+        b_tile(5)
+        sine_of(0)
+        sine_of(1)
+        sine_of(2)
+        add_store(1, 1)
+        y_tile(0, 0, psum_acc, "acc")
+        y_tile(1, 0, psum_acc, "acc")
+        sine_tile(3)
         quantize_h(1, 1)
+        sine_tile(4)
+        sine_tile(5)
+        y_tile(0, 1, psum_d, "d1")
+        round_w3(0, 1, nc.vector.tensor_copy)
+        y_tile(1, 1, psum_d, "d2")
+        round_w3(1, 1, nc.vector.tensor_copy)
+        quantize_w3(0, 1)
         quantize_w3(1, 1)
-        for i in range(N_TILES):
-            y_tile(i, 0)
-            y_tile(i, 1)
-            if i + 3 < N_TILES:
-                b_tile(i + 3)
-                sine_tile(i + 3)
-            out_tile(i)
+        out_tile(0)
+        y_tile(2, 0, psum_acc, "acc")
+        y_tile(2, 1, psum_d, "d1")
+        out_tile(1)
+        y_tile(3, 0, psum_acc, "acc")
+        y_tile(3, 1, psum_d, "d2")
+        sine_of(3)
+        out_tile(2)
+        y_tile(4, 0, psum_acc, "acc")
+        y_tile(4, 1, psum_d, "d1")
+        sine_of(4)
+        out_tile(3)
+        y_tile(5, 0, psum_acc, "acc")
+        y_tile(5, 1, psum_d, "d2")
+        sine_of(5)
+        out_tile(4)
+        out_tile(5)

@@ -21,15 +21,14 @@ P = 128
 PACK = 4
 PASS = P * PACK
 BANK = 512
-QUADS = 4
-LIST_COLS = BANK // 16
+QUADS = P // 32
+PER_COL = 16
 N_TILES = N // P
-W3_CUTS = (0, 512, 768)
+EARLY_TILES = N_TILES // 2
 W1_PIECE = 256
-CAST = 256
-TAB_CUTS = tuple(range(0, T + 1, 512))
-QUARTER = -0.25
-PLANE2 = 8
+W3_CUTS = (0, 512, 768)
+ROUND_COLS = 256
+UPPER_ROWS = 8
 
 
 def tile_list_bag_stability_features_kernel(
@@ -48,129 +47,141 @@ def tile_list_bag_stability_features_kernel(
         def kept(shape, dtype, name):
             return keep.tile(shape, dtype, name=name, align_bytes=64)
 
-        def load_scales(clear, queue, plane, scales, first):
-            rows = PACK * scales.shape[0]
-            clear.memset(plane[:].bitcast(I32), 0)
-            for q in range(QUADS):
-                queue.dma_start(
-                    out=plane[32 * q + first : 32 * q + first + rows, :].bitcast(I32),
-                    in_=scales[:, 4 * q : 4 * q + 4, :].bitcast(I32),
-                )
 
-        def load_scale_rows(clear, plane, scales):
+        def load_one_pass_plane(clear, plane, scales):
             clear.memset(plane[:].bitcast(I32), 0)
             for r in range(PACK):
-                nc.sync.dma_start(out=plane[r:P:32, :].bitcast(I32), in_=scales[0, r:16:PACK, :].bitcast(I32))
+                nc.sync.dma_start(out=plane[r:P:32, :].bitcast(I32), in_=scales[0, r : PACK * QUADS : PACK, :].bitcast(I32))
+
+        def load_two_pass_plane(plane, scales):
+            nc.vector.memset(plane[:].bitcast(I32), 0)
+            for q in range(QUADS):
+                first = 32 * q + UPPER_ROWS
+                nc.sync.dma_start(
+                    out=plane[first : first + 2 * PACK, :].bitcast(I32),
+                    in_=scales[:, PACK * q : PACK * (q + 1), :].bitcast(I32),
+                )
 
         def load_words(tile, words):
             nc.sync.dma_start(out=tile.bitcast(I32), in_=words.rearrange("p t i -> p (t i)").bitcast(I32))
 
-        def load_rows(pool, rows, name, tag):
-            raw = pool.tile([P, PACK, rows.shape[1]], F32, name=name, tag=tag)
+        def load_rows(pool, rows, tag):
+            raw = pool.tile([P, PACK, rows.shape[1]], F32, name="raw", tag=tag)
             nc.sync.dma_start(out=raw[:], in_=rows.rearrange("(p j) c -> p j c", j=PACK))
             return raw
 
+        w1_raw = {}
+        w3_raw = {}
+        store_sb = {}
+
         def load_w1(g):
-            return [
-                load_rows(four, w1[:, g * PASS + e * W1_PIECE : g * PASS + (e + 1) * W1_PIECE], "w1_raw", "w1_raw")
-                for e in range(PASS // W1_PIECE)
-            ]
+            for e in range(PASS // W1_PIECE):
+                first = g * PASS + e * W1_PIECE
+                w1_raw[g, e] = load_rows(four, w1[:, first : first + W1_PIECE], "narrow_raw")
+
+        def load_w3(g, e):
+            pool, tag = ((two, "wide_raw"), (four, "narrow_raw"))[e]
+            w3_raw[g, e] = load_rows(pool, w3[g * PASS : (g + 1) * PASS, W3_CUTS[e] : W3_CUTS[e + 1]], tag)
 
         def load_store(half, g):
             rows = store[g * PASS : (g + 1) * PASS, half * BANK : (half + 1) * BANK]
-            return load_rows(three, rows, "store_sb", "store_sb")
+            store_sb[half, g] = load_rows(three, rows, "store_sb")
 
-        def load_w3(g, e):
-            rows = w3[g * PASS : (g + 1) * PASS, W3_CUTS[e] : W3_CUTS[e + 1]]
-            return load_rows(two, rows, "w3_raw", "w3_raw") if e == 0 else load_rows(four, rows, "w3_raw", "w1_raw")
-
-        idx = kept([P, S // 16], U16, "idx")
-        idx2 = kept([P, B // 16], U16, "idx2")
-        picks = kept([P, B // 16], U16, "picks")
+        idx = kept([P, S // PER_COL], U16, "idx")
+        idx2 = kept([P, B // PER_COL], U16, "idx2")
+        picks = kept([P, B // PER_COL], U16, "picks")
         nc.sync.dma_start(idx[:], offs)
         nc.sync.dma_start(idx2[:], offs2)
         nc.sync.dma_start(picks[:], pos1)
         w2_raw = kept([P, 2 * H], U8, "w2_raw")
         nc.sync.dma_start(out=w2_raw[:].bitcast(I32), in_=w2_words[0].bitcast(I32))
+
         w2_s_raw = kept([P, H], U8, "w2_s_raw")
-        load_scale_rows(nc.vector, w2_s_raw, w2_scales)
+        tab_w = kept([P, T], U32, "tab_w")
+        load_words(tab_w[:, 0 : T // 2], tab_words[0, :, 0 : T // 2, :])
+        load_one_pass_plane(nc.gpsimd, w2_s_raw, w2_scales)
+        load_words(tab_w[:, T // 2 : T], tab_words[0, :, T // 2 : T, :])
+
         warm = kept([P, 1], F32, "warm")
         nc.gpsimd.memset(warm[:], 0.0)
         warm_out = kept([P, 1], F32, "warm_out")
         nc.scalar.activation(out=warm_out[:], in_=warm[:], func=ACT.Sin)
 
-        tab_w = kept([P, T], U32, "tab_w")
-        for e in range(len(TAB_CUTS) - 1):
-            cols = slice(TAB_CUTS[e], TAB_CUTS[e + 1])
-            load_words(tab_w[:, cols], tab_words[0, :, cols, :])
-
         tab_s = kept([P, T], U8, "tab_s")
         tab2_s = kept([P, T2], U8, "tab2_s")
         w4_s = kept([P, N], U8, "w4_s")
-        load_scale_rows(nc.vector, tab_s, tab_scales)
-        w1_raw = [load_w1(0)]
+        load_one_pass_plane(nc.vector, tab_s, tab_scales)
+        load_w1(0)
 
-        store_sb = {}
-        w3_raw = {}
         tab2_w = [kept([P, T2], U32, "tab2_w%d" % a) for a in range(2)]
         w4_w = [kept([P, N], U32, "w4_w%d" % a) for a in range(2)]
-
-        load_scales(nc.vector, nc.sync, tab2_s, tab2_scales, PLANE2)
-        store_sb[0, 0] = load_store(0, 0)
+        load_two_pass_plane(tab2_s, tab2_scales)
+        load_store(0, 0)
         load_words(tab2_w[0][:], tab2_words[0])
-        w1_raw.append(load_w1(1))
+        load_w1(1)
         load_words(tab2_w[1][:], tab2_words[1])
-        load_scales(nc.vector, nc.sync, w4_s, w4_scales, PLANE2)
+        load_two_pass_plane(w4_s, w4_scales)
         for a in range(2):
             load_words(w4_w[a][:], w4_words[a])
-        store_sb[1, 0] = load_store(1, 0)
-        w3_raw[0, 0] = load_w3(0, 0)
-        store_sb[0, 1] = load_store(0, 1)
-        w3_raw[1, 0] = load_w3(1, 0)
+        load_store(1, 0)
+        load_w3(0, 0)
+        load_store(0, 1)
+        load_w3(1, 0)
+
+
         w2_w = kept([P, 2 * H], U8, "w2_w")
         w2_s = kept([P, H], U8, "w2_s")
-        nc.vector.tensor_copy(
-            out=w2_w[:].rearrange("p (g t m b) -> p g t m b", g=2, t=PACK, b=2),
-            in_=w2_raw[:].rearrange("p (g m t b) -> p g t m b", g=2, t=PACK, b=2),
-        )
+
+        def deal_w2_words():
+            nc.vector.tensor_copy(
+                out=w2_w[:].rearrange("p (g t m b) -> p g t m b", g=2, t=PACK, b=2),
+                in_=w2_raw[:].rearrange("p (g m t b) -> p g t m b", g=2, t=PACK, b=2),
+            )
+
+        def deal_w2_scales():
+            nc.vector.tensor_copy(
+                out=w2_s[:].rearrange("p (g t m) -> p g t m", g=2, t=PACK),
+                in_=w2_s_raw[:].rearrange("p (g m t) -> p g t m", g=2, t=PACK),
+            )
 
         v_w = {}
         v_s = {}
 
-        def gather_v(window, half, dtype, tag):
-            picked = keep.tile([P, BANK], dtype, name="picked", tag=tag, align_bytes=64)
-            nc.vector.tensor_copy(picked[:], window[:].indirect(idx[:, half * LIST_COLS : (half + 1) * LIST_COLS]))
-            return picked
+        def gather_v(half):
+            listed = idx[:, half * BANK // PER_COL : (half + 1) * BANK // PER_COL]
+            v_w[half] = kept([P, BANK], U32, "v_w%d" % half)
+            nc.vector.tensor_copy(v_w[half][:], tab_w[:].indirect(listed))
+            v_s[half] = kept([P, BANK], U8, "v_s%d" % half)
+            nc.vector.tensor_copy(v_s[half][:], tab_s[:].indirect(listed))
 
         w1_w = [kept([P, PASS], U32, "w1_w%d" % g) for g in range(2)]
         w1_s = [kept([P, PASS], U8, "w1_s%d" % g) for g in range(2)]
-
         w1_bf = {}
 
-        def round_w1(g, e):
-            if e == 0:
-                w1_bf[g] = keep.tile([P, PACK * PASS], BF16, name="w1_bf", tag="w1_bf%d" % g, align_bytes=64)
-            m = slice(e * W1_PIECE // PACK, (e + 1) * W1_PIECE // PACK)
-            nc.scalar.copy(
-                out=w1_bf[g][:].rearrange("p (t m j) -> p m j t", t=PACK, j=PACK)[:, m, :, :],
-                in_=w1_raw[g][e][:].rearrange("p j (m t) -> p m j t", t=PACK),
-            )
+        def round_w1(g):
+            w1_bf[g] = kept([P, PACK * PASS], BF16, "w1_bf%d" % g)
+            for e in range(PASS // W1_PIECE):
+                places = slice(e * W1_PIECE // PACK, (e + 1) * W1_PIECE // PACK)
+                nc.scalar.copy(
+                    out=w1_bf[g][:].rearrange("p (t m j) -> p m j t", t=PACK, j=PACK)[:, places, :, :],
+                    in_=w1_raw[g, e][:].rearrange("p j (m t) -> p m j t", t=PACK),
+                )
 
         def quantize_w1(g):
             nc.vector.quantize_mx(out=w1_w[g][:].bitcast(FP8X4), scales=w1_s[g][:], in_=w1_bf[g][:])
 
         w3_w = [kept([P, N], U32, "w3_w%d" % g) for g in range(2)]
         w3_s = [kept([P, N], U8, "w3_s%d" % g) for g in range(2)]
-
         w3_bf = {}
 
         def round_w3(g, e, copy):
             width = W3_CUTS[e + 1] - W3_CUTS[e]
-            w3_bf[g, e] = two.tile([P, PACK * width], BF16, name="grouped3", tag="grouped", align_bytes=64)
-            for c0 in range(0, width, CAST):
+            w3_bf[g, e] = two.tile([P, PACK * width], BF16, name="w3_bf", tag="w3_bf", align_bytes=64)
+            for first in range(0, width, ROUND_COLS):
+                last = first + ROUND_COLS
                 copy(
-                    out=w3_bf[g, e][:, PACK * c0 : PACK * (c0 + CAST)].rearrange("p (c i j) -> p c j i", i=4, j=PACK),
-                    in_=w3_raw[g, e][:, :, c0 : c0 + CAST].rearrange("p j (c i) -> p c j i", i=4),
+                    out=w3_bf[g, e][:, PACK * first : PACK * last].rearrange("p (c i j) -> p c j i", i=4, j=PACK),
+                    in_=w3_raw[g, e][:, :, first:last].rearrange("p j (c i) -> p c j i", i=4),
                 )
 
         def quantize_w3(g, e):
@@ -182,25 +193,25 @@ def tile_list_bag_stability_features_kernel(
         h_w = {}
         h_s = {}
 
-        def lesser_slice(half, g, t):
-            if t == 0:
-                lesser[half, g] = three.tile([P, PACK, BANK], F32, name="lesser", tag="lesser")
-            cols = slice(t * P, (t + 1) * P)
-            c = PACK * g + t
-            d1 = psum_d.tile([P, BANK], F32, name="d1", tag="d1")
-            nc.tensor.matmul_mx(
-                out=d1[:], lhsT=w1_w[g][:, cols].bitcast(FP8X4), lhsT_scale=w1_s[g][:, cols],
-                rhs=v_w[half][:].bitcast(FP8X4), rhs_scale=v_s[half][:], start=True, stop=True,
-            )
-            d2 = psum_d.tile([P, BANK], F32, name="d2", tag="d2")
-            nc.tensor.matmul_mx(
-                out=d2[:], lhsT=w2_w[:, 2 * P * c : 2 * P * (c + 1)].bitcast(FP4X4),
-                lhsT_scale=w2_s[:, P * c : P * (c + 1)],
-                rhs=v_w[half][:].bitcast(FP8X4), rhs_scale=v_s[half][:], start=True, stop=True,
-            )
-            row = lesser[half, g][:, t, :]
-            nc.scalar.copy(out=row, in_=d1[:])
-            nc.vector.tensor_tensor(out=row, in0=d2[:], in1=row, op=ALU.min)
+        def lesser_chunk(half, g):
+            lesser[half, g] = three.tile([P, PACK, BANK], F32, name="lesser", tag="lesser")
+            for t in range(PACK):
+                cols = slice(t * P, (t + 1) * P)
+                place = P * (PACK * g + t)
+                d1 = psum_d.tile([P, BANK], F32, name="d1", tag="d1")
+                nc.tensor.matmul_mx(
+                    out=d1[:], lhsT=w1_w[g][:, cols].bitcast(FP8X4), lhsT_scale=w1_s[g][:, cols],
+                    rhs=v_w[half][:].bitcast(FP8X4), rhs_scale=v_s[half][:], start=True, stop=True,
+                )
+                d2 = psum_d.tile([P, BANK], F32, name="d2", tag="d2")
+                nc.tensor.matmul_mx(
+                    out=d2[:], lhsT=w2_w[:, 2 * place : 2 * (place + P)].bitcast(FP4X4),
+                    lhsT_scale=w2_s[:, place : place + P],
+                    rhs=v_w[half][:].bitcast(FP8X4), rhs_scale=v_s[half][:], start=True, stop=True,
+                )
+                row = lesser[half, g][:, t, :]
+                nc.scalar.copy(out=row, in_=d1[:])
+                nc.vector.tensor_tensor(out=row, in0=d2[:], in1=row, op=ALU.min)
 
         def add_store(half, g):
             h_bf[half, g] = two.tile([P, PACK * BANK], BF16, name="h_bf", tag="h_bf", align_bytes=64)
@@ -218,7 +229,8 @@ def tile_list_bag_stability_features_kernel(
 
         y_sb = [kept([P, S], F32, "y%d" % i) for i in range(N_TILES)]
 
-        def y_tile(i, half, pool, tag):
+        def y_half(i, half):
+            pool, tag = ((psum_acc, "acc"), (psum_d, ("d1", "d2")[i % 2]))[half]
             cols = slice(i * P, (i + 1) * P)
             acc = pool.tile([P, BANK], F32, name="y_acc", tag=tag)
             for g in range(2):
@@ -230,125 +242,113 @@ def tile_list_bag_stability_features_kernel(
             nc.scalar.copy(out=y_sb[i][:, half * BANK : (half + 1) * BANK], in_=acc[:])
 
         v2_w = [kept([P, B], U32, "v2_w%d" % a) for a in range(2)]
-        v2_s = {}
 
-        def gather_v2():
+        def gather_v2_scales():
+            picked = keep.tile([P, B], U8, name="v2_s", tag="w1_bf0", align_bytes=64)
+            nc.vector.tensor_copy(picked[:], tab2_s[:].indirect(idx2[:]))
+            return picked
+
+        def gather_v2_words():
             for a in range(2):
                 nc.vector.tensor_copy(v2_w[a][:], tab2_w[a][:].indirect(idx2[:]))
 
-        turns = {}
+        wave = {}
         whole = {}
 
         def b_tile(i):
             cols = slice(i * P, (i + 1) * P)
-            acc = psum_acc.tile([P, BANK], F32, name="acc", tag="acc")
+            acc = psum_acc.tile([P, BANK], F32, name="b_acc", tag="acc")
             for a in range(2):
+                first = UPPER_ROWS + PACK * a
                 nc.tensor.matmul_mx(
-                    out=acc[:], lhsT=w4_w[a][:, cols].bitcast(FP8X4), lhsT_scale=w4_s[PLANE2 + PACK * a : P, cols],
-                    rhs=v2_w[a][:].bitcast(FP8X4), rhs_scale=v2_s[0][PLANE2 + PACK * a : P, :],
+                    out=acc[:], lhsT=w4_w[a][:, cols].bitcast(FP8X4), lhsT_scale=w4_s[first:P, cols],
+                    rhs=v2_w[a][:].bitcast(FP8X4), rhs_scale=v2_s[first:P, :],
                     start=(a == 0), stop=(a == 1),
                 )
-            turns[i] = kept([P, B], F32, "turns%d" % i)
-            nc.scalar.activation(out=turns[i][:], in_=acc[:], func=ACT.Abs, scale=1.0 / (2.0 * math.pi), bias=QUARTER)
+            wave[i] = kept([P, B], F32, "wave%d" % i)
+            nc.scalar.activation(out=wave[i][:], in_=acc[:], func=ACT.Abs, scale=1.0 / (2.0 * math.pi), bias=-0.25)
             whole[i] = three.tile([P, B], U32, name="whole", tag="whole")
-            nc.scalar.activation(out=whole[i][:], in_=turns[i][:], func=ACT.Copy, bias=-0.25)
+            nc.scalar.activation(out=whole[i][:], in_=wave[i][:], func=ACT.Copy, bias=-0.25)
 
-        def sine_tile(i):
-            nc.vector.tensor_tensor(out=turns[i][:], in0=turns[i][:], in1=whole[i][:].bitcast(I32), op=ALU.subtract)
+        def drop_whole_turns(i):
+            nc.vector.tensor_tensor(out=wave[i][:], in0=wave[i][:], in1=whole[i][:].bitcast(I32), op=ALU.subtract)
 
-        def sine_of(i):
-            nc.scalar.activation(out=turns[i][:], in_=turns[i][:], func=ACT.Sin, scale=-2.0 * math.pi, bias=math.pi / 2.0)
+        def sine(i):
+            nc.scalar.activation(out=wave[i][:], in_=wave[i][:], func=ACT.Sin, scale=-2.0 * math.pi, bias=math.pi / 2.0)
 
         def out_tile(i):
-            result = three.tile([P, B], F32, name="result", tag="result" if i < 3 else "whole")
-            nc.vector.tensor_tensor(out=result[:], in0=y_sb[i][:].indirect(picks[:]), in1=turns[i][:], op=ALU.subtract)
-            nc.sync.dma_start(out=out[i * P : (i + 1) * P, :], in_=result[:])
+            result = three.tile([P, B], F32, name="result", tag="result" if i < EARLY_TILES else "whole")
+            parts = 2 if i == N_TILES - 1 else 1
+            width = B // parts
+            for e in range(parts):
+                cols = slice(e * width, (e + 1) * width)
+                listed = picks[:, e * width // PER_COL : (e + 1) * width // PER_COL]
+                nc.vector.tensor_tensor(
+                    out=result[:, cols], in0=y_sb[i][:].indirect(listed), in1=wave[i][:, cols], op=ALU.subtract
+                )
+                nc.sync.dma_start(out=out[i * P : (i + 1) * P, cols], in_=result[:, cols])
 
-        v_w[0] = gather_v(tab_w, 0, U32, "v_w0")
-        v_s[0] = gather_v(tab_s, 0, U8, "v_s0")
-        round_w1(0, 0)
-        round_w1(0, 1)
+
+        early = range(EARLY_TILES)
+        late = range(EARLY_TILES, N_TILES)
+
+        deal_w2_words()
+        gather_v(0)
+        round_w1(0)
         quantize_w1(0)
-        nc.vector.tensor_copy(
-            out=w2_s[:].rearrange("p (g t m) -> p g t m", g=2, t=PACK),
-            in_=w2_s_raw[:].rearrange("p (g m t) -> p g t m", g=2, t=PACK),
-        )
-        v_w[1] = gather_v(tab_w, 1, U32, "v_w1")
-        v_s[1] = gather_v(tab_s, 1, U8, "v_s1")
-        v2_s[0] = keep.tile([P, B], U8, name="v2_s", tag="w1_bf0", align_bytes=64)
-        nc.vector.tensor_copy(v2_s[0][:], tab2_s[:].indirect(idx2[:]))
-        lesser_slice(0, 0, 0)
-        lesser_slice(0, 0, 1)
-        lesser_slice(0, 0, 2)
-        lesser_slice(0, 0, 3)
-        lesser_slice(1, 0, 0)
-        lesser_slice(1, 0, 1)
-        lesser_slice(1, 0, 2)
-        lesser_slice(1, 0, 3)
-        round_w1(1, 0)
-        round_w1(1, 1)
+        deal_w2_scales()
+        gather_v(1)
+        v2_s = gather_v2_scales()
+
+        lesser_chunk(0, 0)
+        lesser_chunk(1, 0)
+        round_w1(1)
         add_store(0, 0)
-        store_sb[1, 1] = load_store(1, 1)
-        w3_raw[0, 1] = load_w3(0, 1)
-        w3_raw[1, 1] = load_w3(1, 1)
+        load_store(1, 1)
+        for g in range(2):
+            load_w3(g, 1)
         quantize_w1(1)
         quantize_h(0, 0)
-        gather_v2()
-        lesser_slice(0, 1, 0)
-        lesser_slice(0, 1, 1)
-        lesser_slice(0, 1, 2)
-        lesser_slice(0, 1, 3)
+        gather_v2_words()
+
+        lesser_chunk(0, 1)
         add_store(1, 0)
         quantize_h(1, 0)
-        lesser_slice(1, 1, 0)
-        lesser_slice(1, 1, 1)
-        lesser_slice(1, 1, 2)
-        lesser_slice(1, 1, 3)
-        b_tile(0)
-        b_tile(1)
-        b_tile(2)
-        round_w3(0, 0, nc.scalar.copy)
-        round_w3(1, 0, nc.scalar.copy)
-        sine_tile(0)
-        sine_tile(1)
-        sine_tile(2)
+        lesser_chunk(1, 1)
+        for i in early:
+            b_tile(i)
+        for g in range(2):
+            round_w3(g, 0, nc.scalar.copy)
+        for i in early:
+            drop_whole_turns(i)
         quantize_w3(0, 0)
         add_store(0, 1)
         quantize_w3(1, 0)
         quantize_h(0, 1)
-        b_tile(3)
-        b_tile(4)
-        b_tile(5)
-        sine_of(0)
-        sine_of(1)
-        sine_of(2)
+        for i in late:
+            b_tile(i)
+        for i in early:
+            sine(i)
+
         add_store(1, 1)
-        y_tile(0, 0, psum_acc, "acc")
-        y_tile(1, 0, psum_acc, "acc")
-        sine_tile(3)
+        y_half(0, 0)
+        y_half(1, 0)
+        drop_whole_turns(late[0])
         quantize_h(1, 1)
-        sine_tile(4)
-        sine_tile(5)
-        y_tile(0, 1, psum_d, "d1")
-        round_w3(0, 1, nc.vector.tensor_copy)
-        y_tile(1, 1, psum_d, "d2")
+        for i in late[1:]:
+            drop_whole_turns(i)
+        y_half(0, 1)
+        round_w3(0, 1, nc.scalar.copy)
+        y_half(1, 1)
         round_w3(1, 1, nc.vector.tensor_copy)
-        quantize_w3(0, 1)
-        quantize_w3(1, 1)
-        out_tile(0)
-        y_tile(2, 0, psum_acc, "acc")
-        y_tile(2, 1, psum_d, "d1")
-        out_tile(1)
-        y_tile(3, 0, psum_acc, "acc")
-        y_tile(3, 1, psum_d, "d2")
-        sine_of(3)
-        out_tile(2)
-        y_tile(4, 0, psum_acc, "acc")
-        y_tile(4, 1, psum_d, "d1")
-        sine_of(4)
-        out_tile(3)
-        y_tile(5, 0, psum_acc, "acc")
-        y_tile(5, 1, psum_d, "d2")
-        sine_of(5)
-        out_tile(4)
-        out_tile(5)
+        for g in range(2):
+            quantize_w3(g, 1)
+
+        for i in range(N_TILES):
+            out_tile(i)
+            ahead = i + 2
+            if ahead < N_TILES:
+                y_half(ahead, 0)
+                y_half(ahead, 1)
+                if ahead in late:
+                    sine(ahead)

import math
from contextlib import ExitStack

import concourse.mybir as mybir

K, K2, H, N, T, T2, S, B = 512, 1024, 1024, 768, 4096, 2048, 1024, 512
FLOPS = 2 * (2 * K * H * S + H * N * S + K2 * N * B)

F32 = mybir.dt.float32
BF16 = mybir.dt.bfloat16
I32 = mybir.dt.int32
U32 = mybir.dt.uint32
U16 = mybir.dt.uint16
U8 = mybir.dt.uint8
FP8X4 = mybir.dt.float8_e4m3fn_x4
FP4X4 = mybir.dt.float4_e2m1fn_x4
ALU = mybir.AluOpType
ACT = mybir.ActivationFunctionType

P = 128
PACK = 4
PASS = P * PACK
BANK = 512
QUADS = P // 32
PER_COL = 16
N_TILES = N // P
EARLY_TILES = N_TILES // 2
W1_PIECE = 256
W3_CUTS = (0, 512, 768)
ROUND_COLS = 256
UPPER_ROWS = 8


def tile_list_bag_stability_features_kernel(
    tc, tab_words, tab_scales, tab2_words, tab2_scales, offs, offs2, pos1,
    w1, w2_words, w2_scales, store, w3, w4_words, w4_scales, out,
):
    nc = tc.nc
    with ExitStack() as ctx:
        keep = ctx.enter_context(tc.tile_pool(name="keep", bufs=1))
        two = ctx.enter_context(tc.tile_pool(name="two", bufs=2))
        three = ctx.enter_context(tc.tile_pool(name="three", bufs=3))
        four = ctx.enter_context(tc.tile_pool(name="four", bufs=4))
        psum_d = ctx.enter_context(tc.psum_pool(name="psum_d", bufs=3))
        psum_acc = ctx.enter_context(tc.psum_pool(name="psum_acc", bufs=2))

        def kept(shape, dtype, name):
            return keep.tile(shape, dtype, name=name, align_bytes=64)


        def load_one_pass_plane(clear, plane, scales):
            clear.memset(plane[:].bitcast(I32), 0)
            for r in range(PACK):
                nc.sync.dma_start(out=plane[r:P:32, :].bitcast(I32), in_=scales[0, r : PACK * QUADS : PACK, :].bitcast(I32))

        def load_two_pass_plane(plane, scales):
            nc.vector.memset(plane[:].bitcast(I32), 0)
            for q in range(QUADS):
                first = 32 * q + UPPER_ROWS
                nc.sync.dma_start(
                    out=plane[first : first + 2 * PACK, :].bitcast(I32),
                    in_=scales[:, PACK * q : PACK * (q + 1), :].bitcast(I32),
                )

        def load_words(tile, words):
            nc.sync.dma_start(out=tile.bitcast(I32), in_=words.rearrange("p t i -> p (t i)").bitcast(I32))

        def load_rows(pool, rows, tag):
            raw = pool.tile([P, PACK, rows.shape[1]], F32, name="raw", tag=tag)
            nc.sync.dma_start(out=raw[:], in_=rows.rearrange("(p j) c -> p j c", j=PACK))
            return raw

        w1_raw = {}
        w3_raw = {}
        store_sb = {}

        def load_w1(g):
            for e in range(PASS // W1_PIECE):
                first = g * PASS + e * W1_PIECE
                w1_raw[g, e] = load_rows(four, w1[:, first : first + W1_PIECE], "narrow_raw")

        def load_w3(g, e):
            pool, tag = ((two, "wide_raw"), (four, "narrow_raw"))[e]
            w3_raw[g, e] = load_rows(pool, w3[g * PASS : (g + 1) * PASS, W3_CUTS[e] : W3_CUTS[e + 1]], tag)

        def load_store(half, g):
            rows = store[g * PASS : (g + 1) * PASS, half * BANK : (half + 1) * BANK]
            store_sb[half, g] = load_rows(three, rows, "store_sb")

        idx = kept([P, S // PER_COL], U16, "idx")
        idx2 = kept([P, B // PER_COL], U16, "idx2")
        picks = kept([P, B // PER_COL], U16, "picks")
        nc.sync.dma_start(idx[:], offs)
        nc.sync.dma_start(idx2[:], offs2)
        nc.sync.dma_start(picks[:], pos1)
        w2_raw = kept([P, 2 * H], U8, "w2_raw")
        nc.sync.dma_start(out=w2_raw[:].bitcast(I32), in_=w2_words[0].bitcast(I32))

        w2_s_raw = kept([P, H], U8, "w2_s_raw")
        tab_w = kept([P, T], U32, "tab_w")
        load_words(tab_w[:, 0 : T // 2], tab_words[0, :, 0 : T // 2, :])
        load_one_pass_plane(nc.gpsimd, w2_s_raw, w2_scales)
        load_words(tab_w[:, T // 2 : T], tab_words[0, :, T // 2 : T, :])

        warm = kept([P, 1], F32, "warm")
        nc.gpsimd.memset(warm[:], 0.0)
        warm_out = kept([P, 1], F32, "warm_out")
        nc.scalar.activation(out=warm_out[:], in_=warm[:], func=ACT.Sin)

        tab_s = kept([P, T], U8, "tab_s")
        tab2_s = kept([P, T2], U8, "tab2_s")
        w4_s = kept([P, N], U8, "w4_s")
        load_one_pass_plane(nc.vector, tab_s, tab_scales)
        load_w1(0)

        tab2_w = [kept([P, T2], U32, "tab2_w%d" % a) for a in range(2)]
        w4_w = [kept([P, N], U32, "w4_w%d" % a) for a in range(2)]
        load_two_pass_plane(tab2_s, tab2_scales)
        load_store(0, 0)
        load_words(tab2_w[0][:], tab2_words[0])
        load_w1(1)
        load_words(tab2_w[1][:], tab2_words[1])
        load_two_pass_plane(w4_s, w4_scales)
        for a in range(2):
            load_words(w4_w[a][:], w4_words[a])
        load_store(1, 0)
        load_w3(0, 0)
        load_store(0, 1)
        load_w3(1, 0)


        w2_w = kept([P, 2 * H], U8, "w2_w")
        w2_s = kept([P, H], U8, "w2_s")

        def deal_w2_words():
            nc.vector.tensor_copy(
                out=w2_w[:].rearrange("p (g t m b) -> p g t m b", g=2, t=PACK, b=2),
                in_=w2_raw[:].rearrange("p (g m t b) -> p g t m b", g=2, t=PACK, b=2),
            )

        def deal_w2_scales():
            nc.vector.tensor_copy(
                out=w2_s[:].rearrange("p (g t m) -> p g t m", g=2, t=PACK),
                in_=w2_s_raw[:].rearrange("p (g m t) -> p g t m", g=2, t=PACK),
            )

        v_w = {}
        v_s = {}

        def gather_v(half):
            listed = idx[:, half * BANK // PER_COL : (half + 1) * BANK // PER_COL]
            v_w[half] = kept([P, BANK], U32, "v_w%d" % half)
            nc.vector.tensor_copy(v_w[half][:], tab_w[:].indirect(listed))
            v_s[half] = kept([P, BANK], U8, "v_s%d" % half)
            nc.vector.tensor_copy(v_s[half][:], tab_s[:].indirect(listed))

        w1_w = [kept([P, PASS], U32, "w1_w%d" % g) for g in range(2)]
        w1_s = [kept([P, PASS], U8, "w1_s%d" % g) for g in range(2)]
        w1_bf = {}

        def round_w1(g):
            w1_bf[g] = kept([P, PACK * PASS], BF16, "w1_bf%d" % g)
            for e in range(PASS // W1_PIECE):
                places = slice(e * W1_PIECE // PACK, (e + 1) * W1_PIECE // PACK)
                nc.scalar.copy(
                    out=w1_bf[g][:].rearrange("p (t m j) -> p m j t", t=PACK, j=PACK)[:, places, :, :],
                    in_=w1_raw[g, e][:].rearrange("p j (m t) -> p m j t", t=PACK),
                )

        def quantize_w1(g):
            nc.vector.quantize_mx(out=w1_w[g][:].bitcast(FP8X4), scales=w1_s[g][:], in_=w1_bf[g][:])

        w3_w = [kept([P, N], U32, "w3_w%d" % g) for g in range(2)]
        w3_s = [kept([P, N], U8, "w3_s%d" % g) for g in range(2)]
        w3_bf = {}

        def round_w3(g, e, copy):
            width = W3_CUTS[e + 1] - W3_CUTS[e]
            w3_bf[g, e] = two.tile([P, PACK * width], BF16, name="w3_bf", tag="w3_bf", align_bytes=64)
            for first in range(0, width, ROUND_COLS):
                last = first + ROUND_COLS
                copy(
                    out=w3_bf[g, e][:, PACK * first : PACK * last].rearrange("p (c i j) -> p c j i", i=4, j=PACK),
                    in_=w3_raw[g, e][:, :, first:last].rearrange("p j (c i) -> p c j i", i=4),
                )

        def quantize_w3(g, e):
            cols = slice(W3_CUTS[e], W3_CUTS[e + 1])
            nc.vector.quantize_mx(out=w3_w[g][:, cols].bitcast(FP8X4), scales=w3_s[g][:, cols], in_=w3_bf[g, e][:])

        lesser = {}
        h_bf = {}
        h_w = {}
        h_s = {}

        def lesser_chunk(half, g):
            lesser[half, g] = three.tile([P, PACK, BANK], F32, name="lesser", tag="lesser")
            for t in range(PACK):
                cols = slice(t * P, (t + 1) * P)
                place = P * (PACK * g + t)
                d1 = psum_d.tile([P, BANK], F32, name="d1", tag="d1")
                nc.tensor.matmul_mx(
                    out=d1[:], lhsT=w1_w[g][:, cols].bitcast(FP8X4), lhsT_scale=w1_s[g][:, cols],
                    rhs=v_w[half][:].bitcast(FP8X4), rhs_scale=v_s[half][:], start=True, stop=True,
                )
                d2 = psum_d.tile([P, BANK], F32, name="d2", tag="d2")
                nc.tensor.matmul_mx(
                    out=d2[:], lhsT=w2_w[:, 2 * place : 2 * (place + P)].bitcast(FP4X4),
                    lhsT_scale=w2_s[:, place : place + P],
                    rhs=v_w[half][:].bitcast(FP8X4), rhs_scale=v_s[half][:], start=True, stop=True,
                )
                row = lesser[half, g][:, t, :]
                nc.scalar.copy(out=row, in_=d1[:])
                nc.vector.tensor_tensor(out=row, in0=d2[:], in1=row, op=ALU.min)

        def add_store(half, g):
            h_bf[half, g] = two.tile([P, PACK * BANK], BF16, name="h_bf", tag="h_bf", align_bytes=64)
            nc.vector.tensor_tensor(
                out=h_bf[half, g][:].rearrange("p (c i t) -> p c t i", i=2, t=PACK),
                in0=lesser[half, g][:].rearrange("p t (c i) -> p c t i", i=2),
                in1=store_sb[half, g][:].rearrange("p t (c i) -> p c t i", i=2),
                op=ALU.add,
            )

        def quantize_h(half, g):
            h_w[half, g] = kept([P, BANK], U32, "h_w%d%d" % (half, g))
            h_s[half, g] = kept([P, BANK], U8, "h_s%d%d" % (half, g))
            nc.vector.quantize_mx(out=h_w[half, g][:].bitcast(FP8X4), scales=h_s[half, g][:], in_=h_bf[half, g][:])

        y_sb = [kept([P, S], F32, "y%d" % i) for i in range(N_TILES)]

        def y_half(i, half):
            pool, tag = ((psum_acc, "acc"), (psum_d, ("d1", "d2")[i % 2]))[half]
            cols = slice(i * P, (i + 1) * P)
            acc = pool.tile([P, BANK], F32, name="y_acc", tag=tag)
            for g in range(2):
                nc.tensor.matmul_mx(
                    out=acc[:], lhsT=w3_w[g][:, cols].bitcast(FP8X4), lhsT_scale=w3_s[g][:, cols],
                    rhs=h_w[half, g][:].bitcast(FP8X4), rhs_scale=h_s[half, g][:],
                    start=(g == 0), stop=(g == 1),
                )
            nc.scalar.copy(out=y_sb[i][:, half * BANK : (half + 1) * BANK], in_=acc[:])

        v2_w = [kept([P, B], U32, "v2_w%d" % a) for a in range(2)]

        def gather_v2_scales():
            picked = keep.tile([P, B], U8, name="v2_s", tag="w1_bf0", align_bytes=64)
            nc.vector.tensor_copy(picked[:], tab2_s[:].indirect(idx2[:]))
            return picked

        def gather_v2_words():
            for a in range(2):
                nc.vector.tensor_copy(v2_w[a][:], tab2_w[a][:].indirect(idx2[:]))

        wave = {}
        whole = {}

        def b_tile(i):
            cols = slice(i * P, (i + 1) * P)
            acc = psum_acc.tile([P, BANK], F32, name="b_acc", tag="acc")
            for a in range(2):
                first = UPPER_ROWS + PACK * a
                nc.tensor.matmul_mx(
                    out=acc[:], lhsT=w4_w[a][:, cols].bitcast(FP8X4), lhsT_scale=w4_s[first:P, cols],
                    rhs=v2_w[a][:].bitcast(FP8X4), rhs_scale=v2_s[first:P, :],
                    start=(a == 0), stop=(a == 1),
                )
            wave[i] = kept([P, B], F32, "wave%d" % i)
            nc.scalar.activation(out=wave[i][:], in_=acc[:], func=ACT.Abs, scale=1.0 / (2.0 * math.pi), bias=-0.25)
            whole[i] = three.tile([P, B], U32, name="whole", tag="whole")
            nc.scalar.activation(out=whole[i][:], in_=wave[i][:], func=ACT.Copy, bias=-0.25)

        def drop_whole_turns(i):
            nc.vector.tensor_tensor(out=wave[i][:], in0=wave[i][:], in1=whole[i][:].bitcast(I32), op=ALU.subtract)

        def sine(i):
            nc.scalar.activation(out=wave[i][:], in_=wave[i][:], func=ACT.Sin, scale=-2.0 * math.pi, bias=math.pi / 2.0)

        def out_tile(i):
            result = three.tile([P, B], F32, name="result", tag="result" if i < EARLY_TILES else "whole")
            parts = 2 if i == N_TILES - 1 else 1
            width = B // parts
            for e in range(parts):
                cols = slice(e * width, (e + 1) * width)
                listed = picks[:, e * width // PER_COL : (e + 1) * width // PER_COL]
                nc.vector.tensor_tensor(
                    out=result[:, cols], in0=y_sb[i][:].indirect(listed), in1=wave[i][:, cols], op=ALU.subtract
                )
                nc.sync.dma_start(out=out[i * P : (i + 1) * P, cols], in_=result[:, cols])


        early = range(EARLY_TILES)
        late = range(EARLY_TILES, N_TILES)

        deal_w2_words()
        gather_v(0)
        round_w1(0)
        quantize_w1(0)
        deal_w2_scales()
        gather_v(1)
        v2_s = gather_v2_scales()

        lesser_chunk(0, 0)
        lesser_chunk(1, 0)
        round_w1(1)
        add_store(0, 0)
        load_store(1, 1)
        for g in range(2):
            load_w3(g, 1)
        quantize_w1(1)
        quantize_h(0, 0)
        gather_v2_words()

        lesser_chunk(0, 1)
        add_store(1, 0)
        quantize_h(1, 0)
        lesser_chunk(1, 1)
        for i in early:
            b_tile(i)
        for g in range(2):
            round_w3(g, 0, nc.scalar.copy)
        for i in early:
            drop_whole_turns(i)
        quantize_w3(0, 0)
        add_store(0, 1)
        quantize_w3(1, 0)
        quantize_h(0, 1)
        for i in late:
            b_tile(i)
        for i in early:
            sine(i)

        add_store(1, 1)
        y_half(0, 0)
        y_half(1, 0)
        drop_whole_turns(late[0])
        quantize_h(1, 1)
        for i in late[1:]:
            drop_whole_turns(i)
        y_half(0, 1)
        round_w3(0, 1, nc.scalar.copy)
        y_half(1, 1)
        round_w3(1, 1, nc.vector.tensor_copy)
        for g in range(2):
            quantize_w3(g, 1)

        for i in range(N_TILES):
            out_tile(i)
            ahead = i + 2
            if ahead < N_TILES:
                y_half(ahead, 0)
                y_half(ahead, 1)
                if ahead in late:
                    sine(ahead)
